import numpy as np
import ml_dtypes


def mxq(x, axis, fmt="e4m3"):
    dtype, down = {"e4m3": (ml_dtypes.float8_e4m3fn, 7), "e5m2": (ml_dtypes.float8_e5m2, 14)}[fmt]
    v = np.moveaxis(np.asarray(x, np.float32).astype(ml_dtypes.bfloat16).astype(np.float64), axis, -1)
    blocks = v.reshape(v.shape[:-1] + (-1, 32))
    amax = np.abs(blocks).max(-1, keepdims=True)
    byte = np.maximum(np.where(amax > 0, np.frexp(amax)[1] - 1 + 127, 0) - down, 1)
    scale = np.exp2(byte - 127.0)
    codes = (blocks / scale).astype(np.float32).astype(dtype).astype(np.float64)
    return np.moveaxis((codes * scale).reshape(v.shape), -1, axis)


WIDE = False


def mx_kscale(k):
    if not WIDE:
        return np.ones(k)
    levels = np.array([10, -10, 5, -5, 0])
    if k % 512:
        return np.exp2(np.random.permutation(np.resize(levels, k // 32))).repeat(32)
    a = np.empty((k // 512, 16))
    for p in range(k // 512):
        a[p, :8] = np.random.permutation(np.resize(levels, 8))
        for g in range(8):
            far = levels[np.abs(levels - a[p, g]) >= 10]
            a[p, g + 8] = far[np.random.randint(len(far))]
    return np.exp2(a.ravel()).repeat(32)


def f64(x):
    return np.asarray(x).astype(np.float64)


def striped(idx):
    return np.tile(idx.reshape(-1, 16).T, (8, 1)).astype(np.uint16)


def unstriped(offs):
    return offs[:16].T.reshape(-1).astype(np.int64)


def pack_weight(w):
    k, n = w.shape
    w = f64(np.asarray(w, np.float32).astype(ml_dtypes.bfloat16)).reshape(k // 32, 32, n)
    amax = np.abs(w).max(1)
    byte = np.clip(np.where(amax > 0, np.frexp(amax)[1] - 1 + 127 - 7, 1), 1, 254)
    scaled = (w * np.exp2(127.0 - byte)[:, None, :]).reshape(k, n).astype(np.float32)
    words = np.ascontiguousarray(scaled.reshape(k // 512, 128, 4, n).transpose(0, 1, 3, 2)).astype(ml_dtypes.float8_e4m3fn).view(np.uint8)
    return words, np.ascontiguousarray(byte.astype(np.uint8).reshape(k // 512, 16, n))


def unpack_weight(words, scales):
    g, p, n, _ = words.shape
    vals = np.ascontiguousarray(words).view(ml_dtypes.float8_e4m3fn).astype(np.float64) * np.repeat(np.exp2(scales.astype(np.float64) - 127.0), 8, axis=1)[..., None]
    return vals.transpose(0, 1, 3, 2).reshape(g * 512, n)

def planes(y):
    n, m = y.shape
    v = y.astype(np.float32).astype(ml_dtypes.bfloat16).astype(np.float64).reshape(n // 32, 32, m)
    top = np.abs(v).max(1)
    byte = np.clip(np.where(top > 0, np.frexp(top)[1] - 1 + 127 - 7, 1), 1, 254)
    codes = (v * np.exp2(127.0 - byte)[:, None, :]).reshape(n, m).astype(np.float32).astype(ml_dtypes.float8_e4m3fn).view(np.uint8)
    words = codes.reshape(n // 512, 128, 4, m).transpose(0, 1, 3, 2)
    return np.ascontiguousarray(words), np.ascontiguousarray(byte.astype(np.uint8).reshape(n // 512, 16, m))


K, T, S, V, H, J, W, G = 512, 2048, 512, 512, 512, 512, 256, 2048


def setup_inputs():
    n = np.random.standard_normal
    s = mx_kscale(K)[:, None]
    u = mx_kscale(S)
    packed_xT = pack_weight(n((K, T)) * s)
    packed_w1 = pack_weight(n((K, H)) / np.sqrt(K) / s)
    packed_w2 = pack_weight(n((K, H)) / np.sqrt(K) / s)
    perm = np.random.permutation(V)
    return {
        "x_words": packed_xT[0],
        "x_scales": packed_xT[1],
        "w1_words": packed_w1[0],
        "w1_scales": packed_w1[1],
        "w2_words": packed_w2[0],
        "w2_scales": packed_w2[1],
        "tab": np.random.uniform(0.4, 1.4, (H, J)).astype(np.float32),
        "ga": (np.random.uniform(0.5, 1.5, (H, 1)) * u[:, None]).astype(np.float32),
        "gb": (np.random.uniform(0.5, 1.5, (H, 1)) / u[:, None]).astype(np.float32),
        "tau": np.random.uniform(0.3, 0.9, (S, 1)).astype(np.float32),
        "offs": striped(np.random.permutation(T)[:S]),
        "two": striped(np.random.permutation(T)[:V]),
        "n1": striped(np.random.randint(0, J, S)),
        "n2": striped(np.random.permutation(S)),
        "n3": striped(perm[:W]),
        "n4": striped(perm[W:]),
        "n5": striped(np.random.randint(0, V, G)),
    }


def reference(x_words, x_scales, w1_words, w1_scales, w2_words, w2_scales, tab, ga, gb, tau, offs, two, n1, n2, n3, n4, n5):
    xq = unpack_weight(x_words, x_scales)[:, unstriped(offs)]
    a = unpack_weight(w1_words, w1_scales).T @ xq
    z = f64(ga) * (a * f64(tab)[:, unstriped(n1)] - (0.5 * a[:, unstriped(n2)]))
    x_two = unpack_weight(x_words, x_scales)[:, unstriped(two)]
    b = unpack_weight(w2_words, w2_scales).T @ x_two
    pb = b[:, unstriped(n4)]
    pa = b[:, unstriped(n3)]
    rb = pb - (0.5 * pa)
    ra = np.sqrt((pa) ** 2 + (pb) ** 2 + 0.25)
    ds = np.zeros((H, V))
    ds[:, unstriped(n3)] = ra
    dt = ds.copy()
    dt[:, unstriped(n4)] = rb
    z2 = f64(gb) * dt
    s = 0.0625 * ((mxq(z, 0, "e4m3").T @ mxq(z2, 0, "e4m3")))
    top = s.max(axis=1, keepdims=True)
    ea = np.exp(f64(tau) * (s[:, unstriped(n5)] - top))
    ms = ea.reshape(S, V, 4).sum(axis=2)
    out_0 = (1.5 * s) / (ms + 0.5)
    return (out_0,) + planes(out_0)

@@ -1,0 +1,274 @@
+from contextlib import ExitStack
+
+import concourse.mybir as mybir
+
+F32 = mybir.dt.float32
+BF16 = mybir.dt.bfloat16
+I32 = mybir.dt.int32
+U32 = mybir.dt.uint32
+U16 = mybir.dt.uint16
+U8 = mybir.dt.uint8
+FP8X4 = mybir.dt.float8_e4m3fn_x4
+ALU = mybir.AluOpType
+ACT = mybir.ActivationFunctionType
+
+P = 128
+PACK = 4
+T = 2048
+N = 512
+HALF = 256
+MEMBERS = 4
+CHUNKS = (64, 128, 128, 128, 64)
+EXP_COLS = 64
+FLOPS = 3 * 2 * 512 * 512 * 512
+
+
+def tile_picked_kqkindgpolaregs_none_po_kernel(
+    tc, x_words, x_scales, w1_words, w1_scales, w2_words, w2_scales, tab, ga, gb, tau,
+    offs, two, n1, n2, n3, n4, n5, out_0, out_1, out_2,
+):
+    nc = tc.nc
+    with ExitStack() as ctx:
+        keep = ctx.enter_context(tc.tile_pool(name="keep", bufs=1))
+        psum = ctx.enter_context(tc.psum_pool(name="psum", bufs=1))
+
+        def sb(name, shape, dtype, tag=""):
+            return keep.tile(shape, dtype, name=name, tag=tag, align_bytes=64)
+
+        def planes(name, shape, dtype):
+            return [sb(f"{name}{j}", shape, dtype) for j in range(PACK)]
+
+        def load_list(name, src):
+            tile = keep.tile(list(src.shape), U16, name=name)
+            nc.sync.dma_start(tile[:], src)
+            return tile
+
+        def load_words(tile, src):
+            nc.sync.dma_start(tile[:].bitcast(I32), src[0].rearrange("p c r -> p (c r)").bitcast(I32))
+
+        def load_scales(queue, tile, src):
+            for q in range(4):
+                rows = src[0, 4 * q : 4 * q + 4, :].bitcast(I32)
+                queue.dma_start(tile[32 * q : 32 * q + 32, :].bitcast(I32), rows.partition_broadcast(8))
+
+        def load_column(name, src):
+            tile = sb(name, [P, PACK], F32)
+            nc.gpsimd.dma_start(tile[:], src.rearrange("(p j) o -> p (j o)", j=PACK))
+            return tile
+
+        xw = sb("xw", [P, T], U32)
+        xs = sb("xs", [P, T], U8)
+        w1w = sb("w1w", [P, N], U32)
+        w1s = sb("w1s", [P, N], U8)
+        w2w = sb("w2w", [P, N], U32)
+        w2s = sb("w2s", [P, N], U8)
+        tabw = planes("tabw", [P, N], F32)
+        tab_rows = tab.rearrange("(p j) c -> p j c", j=PACK)
+
+        n1_t = load_list("n1_t", n1)
+        two_t = load_list("two_t", two)
+        load_scales(nc.sync, xs, x_scales)
+        nc.sync.dma_start(tabw[0][:], tab_rows[:, 0, :])
+        load_words(xw, x_words)
+        load_scales(nc.sync, w2s, w2_scales)
+        load_words(w2w, w2_words)
+        offs_t = load_list("offs_t", offs)
+        nc.sync.dma_start(tabw[1][:], tab_rows[:, 1, :])
+        n3_t = load_list("n3_t", n3)
+        n4_t = load_list("n4_t", n4)
+        load_scales(nc.sync, w1s, w1_scales)
+        load_words(w1w, w1_words)
+        nc.sync.dma_start(tabw[2][:], tab_rows[:, 2, :])
+        nc.sync.dma_start(tabw[3][:], tab_rows[:, 3, :])
+        n2_t = load_list("n2_t", n2)
+        n5_t = load_list("n5_t", n5)
+        ga_t = load_column("ga_t", ga)
+        gb_t = load_column("gb_t", gb)
+        tau_t = load_column("tau_t", tau)
+
+        def deal(name, src, dtype):
+            dst = sb(name, [P, N], dtype)
+            nc.vector.tensor_copy(
+                dst[:].rearrange("p (t m) -> p m t", t=PACK), src[:].rearrange("p (m t) -> p m t", t=PACK)
+            )
+            return dst
+
+        def pick(name, src, lst, dtype):
+            dst = sb(name, [P, N], dtype)
+            nc.vector.tensor_copy(dst[:], src[:].indirect(lst[:]))
+            return dst
+
+        xb_s = pick("xb_s", xs, two_t, U8)
+        xa_s = pick("xa_s", xs, offs_t, U8)
+        xb_w = pick("xb_w", xw, two_t, U32)
+        w2wd = deal("w2wd", w2w, U32)
+        w2sd = deal("w2sd", w2s, U8)
+        xa_w = pick("xa_w", xw, offs_t, U32)
+        w1wd = deal("w1wd", w1w, U32)
+        w1sd = deal("w1sd", w1s, U8)
+
+        def product(name, tag, lw, ls, rw, rs):
+            banks = []
+            for j in range(PACK):
+                bank = psum.tile([P, N], F32, name=f"{name}{j}", tag=f"{tag}{j}")
+                cols = slice(P * j, P * (j + 1))
+                nc.tensor.matmul_mx(
+                    out=bank[:], lhsT=lw[:, cols].bitcast(FP8X4), lhsT_scale=ls[:, cols],
+                    rhs=rw[:].bitcast(FP8X4), rhs_scale=rs[:], start=True, stop=True,
+                )
+                banks.append(bank)
+            return banks
+
+        b_ps = product("b_ps", "bs", w2wd, w2sd, xb_w, xb_s)
+        a_ps = product("a_ps", "a", w1wd, w1sd, xa_w, xa_s)
+
+        tabg = planes("tabg", [P, N], F32)
+
+        def fetch_tab(j):
+            for h in range(2):
+                nc.scalar.activation(
+                    tabg[j][:, HALF * h : HALF * (h + 1)], tabw[j][:].indirect(n1_t[:, 16 * h : 16 * (h + 1)]), ACT.Copy
+                )
+
+        bw = planes("bw", [P, N], F32)
+        pab = planes("pab", [P, N], F32)
+        sq = planes("sq", [P, N], F32)
+        rb = planes("rb", [P, HALF], F32)
+        ss = sb("ss", [P, PACK, HALF], F32)
+        ra = sb("ra", [P, PACK, HALF], F32)
+        dt = planes("dt", [P, N], F32)
+
+        fetch_tab(0)
+        fetch_tab(1)
+        for j in range(PACK):
+            nc.vector.tensor_copy(bw[j][:], b_ps[j][:])
+        for j in range(PACK):
+            nc.scalar.activation(pab[j][:, :HALF], bw[j][:].indirect(n3_t[:]), ACT.Copy)
+            nc.scalar.activation(pab[j][:, HALF:], bw[j][:].indirect(n4_t[:]), ACT.Copy)
+            nc.vector.scalar_tensor_tensor(rb[j][:], pab[j][:, :HALF], -0.5, pab[j][:, HALF:], ALU.mult, ALU.add)
+            nc.vector.tensor_tensor(sq[j][:], pab[j][:], pab[j][:], ALU.mult)
+            nc.vector.scalar_tensor_tensor(ss[:, j, :], sq[j][:, :HALF], 0.25, sq[j][:, HALF:], ALU.add, ALU.add)
+        fetch_tab(2)
+        fetch_tab(3)
+        nc.scalar.activation(dt[0][:].indirect(n4_t[:]), rb[0][:], ACT.Copy)
+        nc.scalar.activation(ra[:], ss[:], ACT.Sqrt)
+        for j in range(1, PACK):
+            nc.scalar.activation(dt[j][:].indirect(n4_t[:]), rb[j][:], ACT.Copy)
+        for j in range(PACK):
+            nc.scalar.activation(dt[j][:].indirect(n3_t[:]), ra[:, j, :], ACT.Copy)
+
+        aw = planes("aw", [P, N], F32)
+        at = planes("at", [P, N], F32)
+        zf = sb("zf", [P, PACK, N], F32)
+        for j in range(PACK):
+            nc.vector.tensor_scalar(aw[j][:], a_ps[j][:], ga_t[:, j : j + 1], -0.5, ALU.mult, ALU.mult)
+            nc.vector.scalar_tensor_tensor(at[j][:], a_ps[j][:], ga_t[:, j : j + 1], tabg[j][:], ALU.mult, ALU.mult)
+            for h in range(2):
+                cols = slice(HALF * h, HALF * (h + 1))
+                nc.vector.tensor_tensor(
+                    zf[:, j, cols], aw[j][:].indirect(n2_t[:, 16 * h : 16 * (h + 1)]), at[j][:, cols], ALU.add
+                )
+        zg = sb("zg", [P, N * PACK], BF16, "stage")
+        nc.vector.tensor_copy(
+            zg[:].rearrange("p (t m j) -> p m j t", t=PACK, j=PACK), zf[:].rearrange("p j (m t) -> p m j t", t=PACK)
+        )
+        zw = sb("zw", [P, N], U32)
+        zs = sb("zs", [P, N], U8)
+        nc.vector.quantize_mx(out=zw[:].bitcast(FP8X4), scales=zs[:], in_=zg[:])
+
+        z2g = sb("z2g", [P, N, PACK], BF16, "stage")
+        for j in range(PACK):
+            nc.vector.tensor_scalar(z2g[:, :, j], dt[j][:], gb_t[:, j : j + 1], None, ALU.mult)
+        z2w = sb("z2w", [P, N], U32)
+        z2s = sb("z2s", [P, N], U8)
+        nc.vector.quantize_mx(out=z2w[:].bitcast(FP8X4), scales=z2s[:], in_=z2g[:].rearrange("p c j -> p (c j)"))
+
+        s_ps = product("s_ps", "bs", zw, zs, z2w, z2s)
+        sw = planes("sw", [P, N], F32)
+        top = sb("top", [P, PACK], F32)
+        shift = sb("shift", [P, PACK], F32)
+        for t in range(PACK):
+            nc.vector.tensor_scalar(sw[t][:], s_ps[t][:], 0.0625, None, ALU.mult, ALU.max, accum_out=top[:, t : t + 1])
+            nc.vector.tensor_scalar(shift[:, t : t + 1], top[:, t : t + 1], tau_t[:, t : t + 1], -1.0, ALU.mult, ALU.mult)
+
+        yw = sb("yw", [P, N], U32)
+        ys = sb("ys", [P, N], U8)
+        out_rows = out_0.rearrange("(p t) v -> p t v", t=PACK)
+        out_words = out_1[0].rearrange("p c r -> p (c r)").bitcast(I32)
+        def round_rows(c, y, width):
+            yg = sb(f"yg{c}", [P, width, PACK], BF16)
+            nc.vector.tensor_copy(
+                yg[:].rearrange("p (v i) t -> p v t i", i=4), y[:].rearrange("p t (v i) -> p v t i", i=4)
+            )
+            return yg
+
+        def quantize_rows(yg, cols):
+            nc.vector.quantize_mx(out=yw[:, cols].bitcast(FP8X4), scales=ys[:, cols], in_=yg[:].rearrange("p v t -> p (v t)"))
+            nc.sync.dma_start(out_words[:, cols], yw[:, cols].bitcast(I32))
+
+        def swapped(ap):
+            return ap.rearrange("p (h v) -> p h v", h=2)[:, ::-1, :]
+
+        c0 = 0
+        last = None
+        for c, width in enumerate(CHUNKS):
+            cols = slice(c0, c0 + width)
+            half = width // 2
+            ea = sb(f"ea{c}", [P, PACK, MEMBERS * width], F32)
+            for e0 in range(0, width, EXP_COLS):
+                for t in range(PACK):
+                    lo = (c0 + e0) * MEMBERS // 16
+                    nc.scalar.activation(
+                        ea[:, t ^ 1, MEMBERS * e0 : MEMBERS * (e0 + EXP_COLS)],
+                        sw[t][:].indirect(n5_t[:, lo : lo + EXP_COLS * MEMBERS // 16]),
+                        ACT.Exp, bias=shift[:, t : t + 1], scale=tau_t[:, t : t + 1],
+                    )
+            pairs = sb(f"pairs{c}", [P, PACK * width, 2], F32, "work")
+            ea4 = ea[:].rearrange("p s (v a b) -> p (s v) a b", a=2, b=2)
+            nc.vector.tensor_tensor(pairs[:], ea4[:, :, 0, :], ea4[:, :, 1, :], ALU.add)
+            if last is not None:
+                yg = round_rows(*last[:3])
+            den = sb(f"den{c}", [P, PACK, width], F32)
+            nc.vector.scalar_tensor_tensor(
+                den[:].rearrange("p s v -> p (s v)"), pairs[:, :, 0], 0.5, pairs[:, :, 1], ALU.add, ALU.add
+            )
+            if last is not None:
+                quantize_rows(yg, last[3])
+            num = sb(f"num{c}", [P, PACK, width], F32, "work")
+
+            def numerator(t):
+                nc.vector.scalar_tensor_tensor(
+                    num[:, t, :], s_ps[t][:, cols], 1.5 * 0.0625, den[:, t ^ 3, :], ALU.mult, ALU.mult
+                )
+
+            d2 = sb(f"d2_{c}", [P, 2, width], F32)
+            nc.vector.tensor_tensor(d2[:], den[:, 0:2, :], den[:, 2:4, :], ALU.mult)
+            numerator(0)
+            d4 = sb(f"d4_{c}", [P, width], F32)
+            nc.vector.tensor_tensor(d4[:], d2[:, 0, :], d2[:, 1, :], ALU.mult)
+            numerator(1)
+            d8 = sb(f"d8_{c}", [P, half], F32)
+            nc.vector.tensor_tensor(d8[:], d4[:, :half], d4[:, half:], ALU.mult)
+            numerator(2)
+            inv8 = sb(f"inv8_{c}", [P, half], F32)
+            nc.vector.reciprocal(inv8[:], d8[:])
+            numerator(3)
+            inv4 = sb(f"inv4_{c}", [P, width], F32)
+            nc.vector.tensor_tensor(
+                inv4[:].rearrange("p (h v) -> p h v", h=2), inv8[:].unsqueeze(1).to_broadcast([P, 2, half]), swapped(d4[:]), ALU.mult
+            )
+            inv2 = sb(f"inv2_{c}", [P, 2, width], F32)
+            nc.vector.tensor_tensor(inv2[:], d2[:], inv4[:].unsqueeze(1).to_broadcast([P, 2, width]), ALU.mult)
+            y = sb(f"y{c}", [P, PACK, width], F32)
+            nc.vector.tensor_tensor(
+                y[:].rearrange("p (h g) v -> p h g v", h=2),
+                num[:].rearrange("p (h g) v -> p h g v", h=2),
+                inv2[:].unsqueeze(1).to_broadcast([P, 2, 2, width]),
+                ALU.mult,
+            )
+            nc.sync.dma_start(out_rows[:, :, cols], y[:])
+            last = (c, y, width, cols)
+            c0 = c0 + width
+        quantize_rows(round_rows(*last[:3]), last[3])
+        for q in range(4):
+            nc.scalar.dma_start(out_2[0, 4 * q : 4 * q + 4, :].bitcast(I32), ys[32 * q : 32 * q + 4, :].bitcast(I32))

@@ -18,7 +18,7 @@ T = 2048
 N = 512
 HALF = 256
 MEMBERS = 4
-CHUNKS = (64, 128, 128, 128, 64)
+CHUNKS = (128, 128, 128, 128)
 EXP_COLS = 64
 FLOPS = 3 * 2 * 512 * 512 * 512
 
@@ -53,12 +53,12 @@ def tile_picked_kqkindgpolaregs_none_po_kernel(
 
         def load_column(name, src):
             tile = sb(name, [P, PACK], F32)
-            nc.gpsimd.dma_start(tile[:], src.rearrange("(p j) o -> p (j o)", j=PACK))
+            nc.sync.dma_start(tile[:], src.rearrange("(p j) o -> p (j o)", j=PACK))
             return tile
 
         xw = sb("xw", [P, T], U32)
         xs = sb("xs", [P, T], U8)
-        w1w = sb("w1w", [P, N], U32)
+        w1w = sb("w1w", [P, N], U32, "after_deal")
         w1s = sb("w1s", [P, N], U8)
         w2w = sb("w2w", [P, N], U32)
         w2s = sb("w2s", [P, N], U8)
@@ -66,31 +66,29 @@ def tile_picked_kqkindgpolaregs_none_po_kernel(
         tab_rows = tab.rearrange("(p j) c -> p j c", j=PACK)
 
         n1_t = load_list("n1_t", n1)
+        nc.sync.dma_start(tabw[0][:], tab_rows[:, 0, :])
         two_t = load_list("two_t", two)
         load_scales(nc.sync, xs, x_scales)
-        nc.sync.dma_start(tabw[0][:], tab_rows[:, 0, :])
+        nc.sync.dma_start(tabw[1][:], tab_rows[:, 1, :])
         load_words(xw, x_words)
         load_scales(nc.sync, w2s, w2_scales)
         load_words(w2w, w2_words)
         offs_t = load_list("offs_t", offs)
-        nc.sync.dma_start(tabw[1][:], tab_rows[:, 1, :])
-        n3_t = load_list("n3_t", n3)
-        n4_t = load_list("n4_t", n4)
-        load_scales(nc.sync, w1s, w1_scales)
-        load_words(w1w, w1_words)
         nc.sync.dma_start(tabw[2][:], tab_rows[:, 2, :])
         nc.sync.dma_start(tabw[3][:], tab_rows[:, 3, :])
-        n2_t = load_list("n2_t", n2)
-        n5_t = load_list("n5_t", n5)
+        n3_t = load_list("n3_t", n3)
+        n4_t = load_list("n4_t", n4)
+        load_words(w1w, w1_words)
+        load_scales(nc.gpsimd, w1s, w1_scales)
         ga_t = load_column("ga_t", ga)
+        n2_t = load_list("n2_t", n2)
         gb_t = load_column("gb_t", gb)
+        n5_t = load_list("n5_t", n5)
         tau_t = load_column("tau_t", tau)
 
-        def deal(name, src, dtype):
-            dst = sb(name, [P, N], dtype)
-            nc.vector.tensor_copy(
-                dst[:].rearrange("p (t m) -> p m t", t=PACK), src[:].rearrange("p (m t) -> p m t", t=PACK)
-            )
+        def deal(copy, order, name, src, dtype, tag=""):
+            dst = sb(name, [P, N], dtype, tag)
+            copy(dst[:].rearrange("p (t m) -> " + order, t=PACK), src[:].rearrange("p (m t) -> " + order, t=PACK))
             return dst
 
         def pick(name, src, lst, dtype):
@@ -101,11 +99,11 @@ def tile_picked_kqkindgpolaregs_none_po_kernel(
         xb_s = pick("xb_s", xs, two_t, U8)
         xa_s = pick("xa_s", xs, offs_t, U8)
         xb_w = pick("xb_w", xw, two_t, U32)
-        w2wd = deal("w2wd", w2w, U32)
-        w2sd = deal("w2sd", w2s, U8)
+        w2sd = deal(nc.vector.tensor_copy, "p m t", "w2sd", w2s, U8)
         xa_w = pick("xa_w", xw, offs_t, U32)
-        w1wd = deal("w1wd", w1w, U32)
-        w1sd = deal("w1sd", w1s, U8)
+        w2wd = deal(nc.scalar.copy, "p m t", "w2wd", w2w, U32)
+        w1sd = deal(nc.gpsimd.tensor_copy, "p t m", "w1sd", w1s, U8, "after_a1")
+        w1wd = deal(nc.gpsimd.tensor_copy, "p t m", "w1wd", w1w, U32, "after_a0")
 
         def product(name, tag, lw, ls, rw, rs):
             banks = []
@@ -131,43 +129,58 @@ def tile_picked_kqkindgpolaregs_none_po_kernel(
                 )
 
         bw = planes("bw", [P, N], F32)
-        pab = planes("pab", [P, N], F32)
-        sq = planes("sq", [P, N], F32)
-        rb = planes("rb", [P, HALF], F32)
-        ss = sb("ss", [P, PACK, HALF], F32)
+        pab = sb("pab", [P, PACK, N], F32)
+        sq = sb("sq", [P, PACK, N], F32, "after_deal")
         ra = sb("ra", [P, PACK, HALF], F32)
         dt = planes("dt", [P, N], F32)
-
-        fetch_tab(0)
-        fetch_tab(1)
-        for j in range(PACK):
-            nc.vector.tensor_copy(bw[j][:], b_ps[j][:])
-        for j in range(PACK):
-            nc.scalar.activation(pab[j][:, :HALF], bw[j][:].indirect(n3_t[:]), ACT.Copy)
-            nc.scalar.activation(pab[j][:, HALF:], bw[j][:].indirect(n4_t[:]), ACT.Copy)
-            nc.vector.scalar_tensor_tensor(rb[j][:], pab[j][:, :HALF], -0.5, pab[j][:, HALF:], ALU.mult, ALU.add)
-            nc.vector.tensor_tensor(sq[j][:], pab[j][:], pab[j][:], ALU.mult)
-            nc.vector.scalar_tensor_tensor(ss[:, j, :], sq[j][:, :HALF], 0.25, sq[j][:, HALF:], ALU.add, ALU.add)
-        fetch_tab(2)
-        fetch_tab(3)
-        nc.scalar.activation(dt[0][:].indirect(n4_t[:]), rb[0][:], ACT.Copy)
-        nc.scalar.activation(ra[:], ss[:], ACT.Sqrt)
-        for j in range(1, PACK):
-            nc.scalar.activation(dt[j][:].indirect(n4_t[:]), rb[j][:], ACT.Copy)
-        for j in range(PACK):
-            nc.scalar.activation(dt[j][:].indirect(n3_t[:]), ra[:, j, :], ACT.Copy)
-
         aw = planes("aw", [P, N], F32)
         at = planes("at", [P, N], F32)
         zf = sb("zf", [P, PACK, N], F32)
+
         for j in range(PACK):
+            fetch_tab(j)
+        for j in range(PACK):
+            nc.vector.tensor_copy(bw[j][:], b_ps[j][:])
+        for j in range(PACK):
+            nc.scalar.activation(pab[:, j, :HALF], bw[j][:].indirect(n3_t[:]), ACT.Copy)
+            nc.scalar.activation(pab[:, j, HALF:], bw[j][:].indirect(n4_t[:]), ACT.Copy)
+            if j < PACK - 1:
+                nc.gpsimd.tensor_tensor(sq[:, j, :], pab[:, j, :], pab[:, j, :], ALU.mult)
+
+        rb = sb("rb", [P, PACK, HALF], F32, "after_a0")
+        ss = sb("ss", [P, PACK, HALF], F32, "after_a1")
+
+        def weigh_a(j):
             nc.vector.tensor_scalar(aw[j][:], a_ps[j][:], ga_t[:, j : j + 1], -0.5, ALU.mult, ALU.mult)
             nc.vector.scalar_tensor_tensor(at[j][:], a_ps[j][:], ga_t[:, j : j + 1], tabg[j][:], ALU.mult, ALU.mult)
+
+        def differences(js):
+            nc.vector.scalar_tensor_tensor(rb[:, js, :], pab[:, js, :HALF], -0.5, pab[:, js, HALF:], ALU.mult, ALU.add)
+
+        def mix_a(j):
             for h in range(2):
                 cols = slice(HALF * h, HALF * (h + 1))
                 nc.vector.tensor_tensor(
                     zf[:, j, cols], aw[j][:].indirect(n2_t[:, 16 * h : 16 * (h + 1)]), at[j][:, cols], ALU.add
                 )
+
+        weigh_a(0)
+        differences(slice(0, 2))
+        weigh_a(1)
+        weigh_a(2)
+        differences(slice(2, 4))
+        nc.vector.tensor_tensor(sq[:, PACK - 1, :], pab[:, PACK - 1, :], pab[:, PACK - 1, :], ALU.mult)
+        weigh_a(3)
+        nc.vector.scalar_tensor_tensor(ss[:], sq[:, :, :HALF], 0.25, sq[:, :, HALF:], ALU.add, ALU.add)
+        for j in range(PACK):
+            mix_a(j)
+
+        for j in range(PACK):
+            nc.scalar.activation(dt[j][:].indirect(n4_t[:]), rb[:, j, :], ACT.Copy)
+        nc.scalar.activation(ra[:], ss[:], ACT.Sqrt)
+        for j in range(PACK):
+            nc.scalar.activation(dt[j][:].indirect(n3_t[:]), ra[:, j, :], ACT.Copy)
+
         zg = sb("zg", [P, N * PACK], BF16, "stage")
         nc.vector.tensor_copy(
             zg[:].rearrange("p (t m j) -> p m j t", t=PACK, j=PACK), zf[:].rearrange("p j (m t) -> p m j t", t=PACK)
@@ -177,13 +190,31 @@ def tile_picked_kqkindgpolaregs_none_po_kernel(
         nc.vector.quantize_mx(out=zw[:].bitcast(FP8X4), scales=zs[:], in_=zg[:])
 
         z2g = sb("z2g", [P, N, PACK], BF16, "stage")
-        for j in range(PACK):
+        for j in range(PACK - 1):
             nc.vector.tensor_scalar(z2g[:, :, j], dt[j][:], gb_t[:, j : j + 1], None, ALU.mult)
+        for h in range(2):
+            cols = slice(HALF * h, HALF * (h + 1))
+            nc.vector.tensor_scalar(z2g[:, cols, PACK - 1], dt[PACK - 1][:, cols], gb_t[:, PACK - 1 : PACK], None, ALU.mult)
         z2w = sb("z2w", [P, N], U32)
         z2s = sb("z2s", [P, N], U8)
-        nc.vector.quantize_mx(out=z2w[:].bitcast(FP8X4), scales=z2s[:], in_=z2g[:].rearrange("p c j -> p (c j)"))
+        for h in range(2):
+            cols = slice(HALF * h, HALF * (h + 1))
+            nc.vector.quantize_mx(
+                out=z2w[:, cols].bitcast(FP8X4), scales=z2s[:, cols], in_=z2g[:, cols, :].rearrange("p c j -> p (c j)")
+            )
 
-        s_ps = product("s_ps", "bs", zw, zs, z2w, z2s)
+        s_ps = []
+        for t in range(PACK):
+            bank = psum.tile([P, N], F32, name=f"s_ps{t}", tag=f"bs{t}")
+            rows = slice(P * t, P * (t + 1))
+            step = HALF if t == 0 else N
+            for v0 in range(0, N, step):
+                cols = slice(v0, v0 + step)
+                nc.tensor.matmul_mx(
+                    out=bank[:, cols], lhsT=zw[:, rows].bitcast(FP8X4), lhsT_scale=zs[:, rows],
+                    rhs=z2w[:, cols].bitcast(FP8X4), rhs_scale=z2s[:, cols], start=True, stop=True,
+                )
+            s_ps.append(bank)
         sw = planes("sw", [P, N], F32)
         top = sb("top", [P, PACK], F32)
         shift = sb("shift", [P, PACK], F32)
@@ -195,9 +226,9 @@ def tile_picked_kqkindgpolaregs_none_po_kernel(
         ys = sb("ys", [P, N], U8)
         out_rows = out_0.rearrange("(p t) v -> p t v", t=PACK)
         out_words = out_1[0].rearrange("p c r -> p (c r)").bitcast(I32)
-        def round_rows(c, y, width):
+        def round_rows(copy, c, y, width):
             yg = sb(f"yg{c}", [P, width, PACK], BF16)
-            nc.vector.tensor_copy(
+            copy(
                 yg[:].rearrange("p (v i) t -> p v t i", i=4), y[:].rearrange("p t (v i) -> p v t i", i=4)
             )
             return yg
@@ -206,14 +237,12 @@ def tile_picked_kqkindgpolaregs_none_po_kernel(
             nc.vector.quantize_mx(out=yw[:, cols].bitcast(FP8X4), scales=ys[:, cols], in_=yg[:].rearrange("p v t -> p (v t)"))
             nc.sync.dma_start(out_words[:, cols], yw[:, cols].bitcast(I32))
 
-        def swapped(ap):
-            return ap.rearrange("p (h v) -> p h v", h=2)[:, ::-1, :]
-
         c0 = 0
         last = None
         for c, width in enumerate(CHUNKS):
             cols = slice(c0, c0 + width)
             half = width // 2
+            halves = [slice(0, half), slice(half, width)]
             ea = sb(f"ea{c}", [P, PACK, MEMBERS * width], F32)
             for e0 in range(0, width, EXP_COLS):
                 for t in range(PACK):
@@ -223,52 +252,72 @@ def tile_picked_kqkindgpolaregs_none_po_kernel(
                         sw[t][:].indirect(n5_t[:, lo : lo + EXP_COLS * MEMBERS // 16]),
                         ACT.Exp, bias=shift[:, t : t + 1], scale=tau_t[:, t : t + 1],
                     )
-            pairs = sb(f"pairs{c}", [P, PACK * width, 2], F32, "work")
-            ea4 = ea[:].rearrange("p s (v a b) -> p (s v) a b", a=2, b=2)
-            nc.vector.tensor_tensor(pairs[:], ea4[:, :, 0, :], ea4[:, :, 1, :], ALU.add)
+            pairs = sb(f"pairs{c}", [P, 2, PACK * half, 2], F32, "work")
+            den = sb(f"den{c}", [P, 2, PACK, half], F32)
+            d2 = sb(f"d2_{c}", [P, 2, 2, half], F32)
+            d4 = sb(f"d4_{c}", [P, 2, half], F32)
+            inv4 = sb(f"inv4_{c}", [P, 2, half], F32)
+            inv2 = sb(f"inv2_{c}", [P, 2, 2, half], F32)
+            y = sb(f"y{c}", [P, PACK, width], F32)
+
+            def add_pairs(h):
+                ea4 = ea[:].rearrange("p s (v a b) -> p s v a b", a=2, b=2)[:, :, halves[h], :, :]
+                nc.vector.tensor_tensor(
+                    pairs[:, h, :, :].rearrange("p (s v) b -> p s v b", s=PACK), ea4[:, :, :, 0, :], ea4[:, :, :, 1, :], ALU.add
+                )
+
+            def add_rest(h):
+                nc.vector.scalar_tensor_tensor(
+                    den[:, h, :, :].rearrange("p s v -> p (s v)"), pairs[:, h, :, 0], 0.5, pairs[:, h, :, 1], ALU.add, ALU.add
+                )
+
+            add_pairs(0)
             if last is not None:
-                yg = round_rows(*last[:3])
-            den = sb(f"den{c}", [P, PACK, width], F32)
-            nc.vector.scalar_tensor_tensor(
-                den[:].rearrange("p s v -> p (s v)"), pairs[:, :, 0], 0.5, pairs[:, :, 1], ALU.add, ALU.add
-            )
+                yg = round_rows(nc.scalar.copy if c == len(CHUNKS) - 1 else nc.vector.tensor_copy, *last[:3])
+            add_rest(0)
+            add_pairs(1)
             if last is not None:
                 quantize_rows(yg, last[3])
+            nc.vector.tensor_tensor(d2[:, 0, :, :], den[:, 0, 0:2, :], den[:, 0, 2:4, :], ALU.mult)
+            add_rest(1)
+            nc.vector.tensor_tensor(d4[:, 0, :], d2[:, 0, 0, :], d2[:, 0, 1, :], ALU.mult)
             num = sb(f"num{c}", [P, PACK, width], F32, "work")
 
             def numerator(t):
                 nc.vector.scalar_tensor_tensor(
-                    num[:, t, :], s_ps[t][:, cols], 1.5 * 0.0625, den[:, t ^ 3, :], ALU.mult, ALU.mult
+                    num[:, t, :].rearrange("p (h v) -> p h v", h=2),
+                    s_ps[t][:, cols].rearrange("p (h v) -> p h v", h=2),
+                    1.5 * 0.0625, den[:, :, t ^ 3, :], ALU.mult, ALU.mult,
                 )
 
-            d2 = sb(f"d2_{c}", [P, 2, width], F32)
-            nc.vector.tensor_tensor(d2[:], den[:, 0:2, :], den[:, 2:4, :], ALU.mult)
+            def finish(h):
+                nc.vector.tensor_tensor(
+                    y[:, :, halves[h]].rearrange("p (u g) v -> p u g v", u=2),
+                    num[:, :, halves[h]].rearrange("p (u g) v -> p u g v", u=2),
+                    inv2[:, h, :, :].unsqueeze(1).to_broadcast([P, 2, 2, half]),
+                    ALU.mult,
+                )
+
+            def spread(h):
+                nc.vector.tensor_tensor(
+                    inv2[:, h, :, :], d2[:, h, :, :], inv4[:, h, :].unsqueeze(1).to_broadcast([P, 2, half]), ALU.mult
+                )
+
+            nc.vector.tensor_tensor(d2[:, 1, :, :], den[:, 1, 0:2, :], den[:, 1, 2:4, :], ALU.mult)
             numerator(0)
-            d4 = sb(f"d4_{c}", [P, width], F32)
-            nc.vector.tensor_tensor(d4[:], d2[:, 0, :], d2[:, 1, :], ALU.mult)
+            nc.vector.reciprocal(inv4[:, 0, :], d4[:, 0, :])
+            nc.vector.tensor_tensor(d4[:, 1, :], d2[:, 1, 0, :], d2[:, 1, 1, :], ALU.mult)
             numerator(1)
-            d8 = sb(f"d8_{c}", [P, half], F32)
-            nc.vector.tensor_tensor(d8[:], d4[:, :half], d4[:, half:], ALU.mult)
+            spread(0)
+            nc.vector.reciprocal(inv4[:, 1, :], d4[:, 1, :])
             numerator(2)
-            inv8 = sb(f"inv8_{c}", [P, half], F32)
-            nc.vector.reciprocal(inv8[:], d8[:])
             numerator(3)
-            inv4 = sb(f"inv4_{c}", [P, width], F32)
-            nc.vector.tensor_tensor(
-                inv4[:].rearrange("p (h v) -> p h v", h=2), inv8[:].unsqueeze(1).to_broadcast([P, 2, half]), swapped(d4[:]), ALU.mult
-            )
-            inv2 = sb(f"inv2_{c}", [P, 2, width], F32)
-            nc.vector.tensor_tensor(inv2[:], d2[:], inv4[:].unsqueeze(1).to_broadcast([P, 2, width]), ALU.mult)
-            y = sb(f"y{c}", [P, PACK, width], F32)
-            nc.vector.tensor_tensor(
-                y[:].rearrange("p (h g) v -> p h g v", h=2),
-                num[:].rearrange("p (h g) v -> p h g v", h=2),
-                inv2[:].unsqueeze(1).to_broadcast([P, 2, 2, width]),
-                ALU.mult,
-            )
+            spread(1)
+            finish(0)
+            finish(1)
             nc.sync.dma_start(out_rows[:, :, cols], y[:])
             last = (c, y, width, cols)
             c0 = c0 + width
-        quantize_rows(round_rows(*last[:3]), last[3])
+        quantize_rows(round_rows(nc.vector.tensor_copy, *last[:3]), last[3])
         for q in range(4):
             nc.scalar.dma_start(out_2[0, 4 * q : 4 * q + 4, :].bitcast(I32), ys[32 * q : 32 * q + 4, :].bitcast(I32))

@@ -69,8 +69,8 @@ def tile_picked_kqkindgpolaregs_none_po_kernel(
         nc.sync.dma_start(tabw[0][:], tab_rows[:, 0, :])
         two_t = load_list("two_t", two)
         load_scales(nc.sync, xs, x_scales)
-        nc.sync.dma_start(tabw[1][:], tab_rows[:, 1, :])
         load_words(xw, x_words)
+        nc.sync.dma_start(tabw[1][:], tab_rows[:, 1, :])
         load_scales(nc.sync, w2s, w2_scales)
         load_words(w2w, w2_words)
         offs_t = load_list("offs_t", offs)
@@ -100,8 +100,8 @@ def tile_picked_kqkindgpolaregs_none_po_kernel(
         xa_s = pick("xa_s", xs, offs_t, U8)
         xb_w = pick("xb_w", xw, two_t, U32)
         w2sd = deal(nc.vector.tensor_copy, "p m t", "w2sd", w2s, U8)
+        w2wd = deal(nc.vector.tensor_copy, "p m t", "w2wd", w2w, U32)
         xa_w = pick("xa_w", xw, offs_t, U32)
-        w2wd = deal(nc.scalar.copy, "p m t", "w2wd", w2w, U32)
         w1sd = deal(nc.gpsimd.tensor_copy, "p t m", "w1sd", w1s, U8, "after_a1")
         w1wd = deal(nc.gpsimd.tensor_copy, "p t m", "w1wd", w1w, U32, "after_a0")
 
@@ -135,7 +135,6 @@ def tile_picked_kqkindgpolaregs_none_po_kernel(
         dt = planes("dt", [P, N], F32)
         aw = planes("aw", [P, N], F32)
         at = planes("at", [P, N], F32)
-        zf = sb("zf", [P, PACK, N], F32)
 
         for j in range(PACK):
             fetch_tab(j)
@@ -172,6 +171,7 @@ def tile_picked_kqkindgpolaregs_none_po_kernel(
         nc.vector.tensor_tensor(sq[:, PACK - 1, :], pab[:, PACK - 1, :], pab[:, PACK - 1, :], ALU.mult)
         weigh_a(3)
         nc.vector.scalar_tensor_tensor(ss[:], sq[:, :, :HALF], 0.25, sq[:, :, HALF:], ALU.add, ALU.add)
+        zf = sb("zf", [P, PACK, N], F32, "after_deal")
         for j in range(PACK):
             mix_a(j)
 

@@ -96,6 +96,11 @@ def tile_picked_kqkindgpolaregs_none_po_kernel(
             nc.vector.tensor_copy(dst[:], src[:].indirect(lst[:]))
             return dst
 
+        warm_in = sb("warm_in", [P, 1], F32)
+        warm_out = sb("warm_out", [P, 1], F32)
+        nc.vector.memset(warm_in[:], 1.0)
+        nc.scalar.activation(warm_out[:], warm_in[:], ACT.Sqrt)
+
         xb_s = pick("xb_s", xs, two_t, U8)
         xa_s = pick("xa_s", xs, offs_t, U8)
         xb_w = pick("xb_w", xw, two_t, U32)

@@ -150,6 +150,8 @@ def tile_picked_kqkindgpolaregs_none_po_kernel(
             nc.scalar.activation(pab[:, j, HALF:], bw[j][:].indirect(n4_t[:]), ACT.Copy)
             if j < PACK - 1:
                 nc.gpsimd.tensor_tensor(sq[:, j, :], pab[:, j, :], pab[:, j, :], ALU.mult)
+            else:
+                nc.scalar.activation(sq[:, j, :], pab[:, j, :], ACT.Square)
 
         rb = sb("rb", [P, PACK, HALF], F32, "after_a0")
         ss = sb("ss", [P, PACK, HALF], F32, "after_a1")
@@ -169,11 +171,10 @@ def tile_picked_kqkindgpolaregs_none_po_kernel(
                 )
 
         weigh_a(0)
-        differences(slice(0, 2))
         weigh_a(1)
+        differences(slice(0, 2))
         weigh_a(2)
         differences(slice(2, 4))
-        nc.vector.tensor_tensor(sq[:, PACK - 1, :], pab[:, PACK - 1, :], pab[:, PACK - 1, :], ALU.mult)
         weigh_a(3)
         nc.vector.scalar_tensor_tensor(ss[:], sq[:, :, :HALF], 0.25, sq[:, :, HALF:], ALU.add, ALU.add)
         zf = sb("zf", [P, PACK, N], F32, "after_deal")

from contextlib import ExitStack

import concourse.mybir as mybir

F32 = mybir.dt.float32
BF16 = mybir.dt.bfloat16
I32 = mybir.dt.int32
U32 = mybir.dt.uint32
U16 = mybir.dt.uint16
U8 = mybir.dt.uint8
FP8X4 = mybir.dt.float8_e4m3fn_x4
ALU = mybir.AluOpType
ACT = mybir.ActivationFunctionType

P = 128
PACK = 4
T = 2048
N = 512
HALF = 256
MEMBERS = 4
CHUNKS = (128, 128, 128, 128)
EXP_COLS = 64
FLOPS = 3 * 2 * 512 * 512 * 512


def tile_picked_kqkindgpolaregs_none_po_kernel(
    tc, x_words, x_scales, w1_words, w1_scales, w2_words, w2_scales, tab, ga, gb, tau,
    offs, two, n1, n2, n3, n4, n5, out_0, out_1, out_2,
):
    nc = tc.nc
    with ExitStack() as ctx:
        keep = ctx.enter_context(tc.tile_pool(name="keep", bufs=1))
        psum = ctx.enter_context(tc.psum_pool(name="psum", bufs=1))

        def sb(name, shape, dtype, tag=""):
            return keep.tile(shape, dtype, name=name, tag=tag, align_bytes=64)

        def planes(name, shape, dtype):
            return [sb(f"{name}{j}", shape, dtype) for j in range(PACK)]

        def load_list(name, src):
            tile = keep.tile(list(src.shape), U16, name=name)
            nc.sync.dma_start(tile[:], src)
            return tile

        def load_words(tile, src):
            nc.sync.dma_start(tile[:].bitcast(I32), src[0].rearrange("p c r -> p (c r)").bitcast(I32))

        def load_scales(queue, tile, src):
            for q in range(4):
                rows = src[0, 4 * q : 4 * q + 4, :].bitcast(I32)
                queue.dma_start(tile[32 * q : 32 * q + 32, :].bitcast(I32), rows.partition_broadcast(8))

        def load_column(name, src):
            tile = sb(name, [P, PACK], F32)
            nc.sync.dma_start(tile[:], src.rearrange("(p j) o -> p (j o)", j=PACK))
            return tile

        xw = sb("xw", [P, T], U32)
        xs = sb("xs", [P, T], U8)
        w1w = sb("w1w", [P, N], U32, "after_deal")
        w1s = sb("w1s", [P, N], U8)
        w2w = sb("w2w", [P, N], U32)
        w2s = sb("w2s", [P, N], U8)
        tabw = planes("tabw", [P, N], F32)
        tab_rows = tab.rearrange("(p j) c -> p j c", j=PACK)

        n1_t = load_list("n1_t", n1)
        nc.sync.dma_start(tabw[0][:], tab_rows[:, 0, :])
        two_t = load_list("two_t", two)
        load_scales(nc.sync, xs, x_scales)
        load_words(xw, x_words)
        nc.sync.dma_start(tabw[1][:], tab_rows[:, 1, :])
        load_scales(nc.sync, w2s, w2_scales)
        load_words(w2w, w2_words)
        offs_t = load_list("offs_t", offs)
        nc.sync.dma_start(tabw[2][:], tab_rows[:, 2, :])
        nc.sync.dma_start(tabw[3][:], tab_rows[:, 3, :])
        n3_t = load_list("n3_t", n3)
        n4_t = load_list("n4_t", n4)
        load_words(w1w, w1_words)
        load_scales(nc.gpsimd, w1s, w1_scales)
        ga_t = load_column("ga_t", ga)
        n2_t = load_list("n2_t", n2)
        gb_t = load_column("gb_t", gb)
        n5_t = load_list("n5_t", n5)
        tau_t = load_column("tau_t", tau)

        def deal(copy, order, name, src, dtype, tag=""):
            dst = sb(name, [P, N], dtype, tag)
            copy(dst[:].rearrange("p (t m) -> " + order, t=PACK), src[:].rearrange("p (m t) -> " + order, t=PACK))
            return dst

        def pick(name, src, lst, dtype):
            dst = sb(name, [P, N], dtype)
            nc.vector.tensor_copy(dst[:], src[:].indirect(lst[:]))
            return dst

        warm_in = sb("warm_in", [P, 1], F32)
        warm_out = sb("warm_out", [P, 1], F32)
        nc.vector.memset(warm_in[:], 1.0)
        nc.scalar.activation(warm_out[:], warm_in[:], ACT.Sqrt)

        xb_s = pick("xb_s", xs, two_t, U8)
        xa_s = pick("xa_s", xs, offs_t, U8)
        xb_w = pick("xb_w", xw, two_t, U32)
        w2sd = deal(nc.vector.tensor_copy, "p m t", "w2sd", w2s, U8)
        w2wd = deal(nc.vector.tensor_copy, "p m t", "w2wd", w2w, U32)
        xa_w = pick("xa_w", xw, offs_t, U32)
        w1sd = deal(nc.gpsimd.tensor_copy, "p t m", "w1sd", w1s, U8, "after_a1")
        w1wd = deal(nc.gpsimd.tensor_copy, "p t m", "w1wd", w1w, U32, "after_a0")

        def product(name, tag, lw, ls, rw, rs):
            banks = []
            for j in range(PACK):
                bank = psum.tile([P, N], F32, name=f"{name}{j}", tag=f"{tag}{j}")
                cols = slice(P * j, P * (j + 1))
                nc.tensor.matmul_mx(
                    out=bank[:], lhsT=lw[:, cols].bitcast(FP8X4), lhsT_scale=ls[:, cols],
                    rhs=rw[:].bitcast(FP8X4), rhs_scale=rs[:], start=True, stop=True,
                )
                banks.append(bank)
            return banks

        b_ps = product("b_ps", "bs", w2wd, w2sd, xb_w, xb_s)
        a_ps = product("a_ps", "a", w1wd, w1sd, xa_w, xa_s)

        tabg = planes("tabg", [P, N], F32)

        def fetch_tab(j):
            for h in range(2):
                nc.scalar.activation(
                    tabg[j][:, HALF * h : HALF * (h + 1)], tabw[j][:].indirect(n1_t[:, 16 * h : 16 * (h + 1)]), ACT.Copy
                )

        bw = planes("bw", [P, N], F32)
        pab = sb("pab", [P, PACK, N], F32)
        sq = sb("sq", [P, PACK, N], F32, "after_deal")
        ra = sb("ra", [P, PACK, HALF], F32)
        dt = planes("dt", [P, N], F32)
        aw = planes("aw", [P, N], F32)
        at = planes("at", [P, N], F32)

        for j in range(PACK):
            fetch_tab(j)
        for j in range(PACK):
            nc.vector.tensor_copy(bw[j][:], b_ps[j][:])
        for j in range(PACK):
            nc.scalar.activation(pab[:, j, :HALF], bw[j][:].indirect(n3_t[:]), ACT.Copy)
            nc.scalar.activation(pab[:, j, HALF:], bw[j][:].indirect(n4_t[:]), ACT.Copy)
            if j < PACK - 1:
                nc.gpsimd.tensor_tensor(sq[:, j, :], pab[:, j, :], pab[:, j, :], ALU.mult)
            else:
                nc.scalar.activation(sq[:, j, :], pab[:, j, :], ACT.Square)

        rb = sb("rb", [P, PACK, HALF], F32, "after_a0")
        ss = sb("ss", [P, PACK, HALF], F32, "after_a1")

        def weigh_a(j):
            nc.vector.tensor_scalar(aw[j][:], a_ps[j][:], ga_t[:, j : j + 1], -0.5, ALU.mult, ALU.mult)
            nc.vector.scalar_tensor_tensor(at[j][:], a_ps[j][:], ga_t[:, j : j + 1], tabg[j][:], ALU.mult, ALU.mult)

        def differences(js):
            nc.vector.scalar_tensor_tensor(rb[:, js, :], pab[:, js, :HALF], -0.5, pab[:, js, HALF:], ALU.mult, ALU.add)

        def mix_a(j):
            for h in range(2):
                cols = slice(HALF * h, HALF * (h + 1))
                nc.vector.tensor_tensor(
                    zf[:, j, cols], aw[j][:].indirect(n2_t[:, 16 * h : 16 * (h + 1)]), at[j][:, cols], ALU.add
                )

        weigh_a(0)
        weigh_a(1)
        differences(slice(0, 2))
        weigh_a(2)
        differences(slice(2, 4))
        weigh_a(3)
        nc.vector.scalar_tensor_tensor(ss[:], sq[:, :, :HALF], 0.25, sq[:, :, HALF:], ALU.add, ALU.add)
        zf = sb("zf", [P, PACK, N], F32, "after_deal")
        for j in range(PACK):
            mix_a(j)

        for j in range(PACK):
            nc.scalar.activation(dt[j][:].indirect(n4_t[:]), rb[:, j, :], ACT.Copy)
        nc.scalar.activation(ra[:], ss[:], ACT.Sqrt)
        for j in range(PACK):
            nc.scalar.activation(dt[j][:].indirect(n3_t[:]), ra[:, j, :], ACT.Copy)

        zg = sb("zg", [P, N * PACK], BF16, "stage")
        nc.vector.tensor_copy(
            zg[:].rearrange("p (t m j) -> p m j t", t=PACK, j=PACK), zf[:].rearrange("p j (m t) -> p m j t", t=PACK)
        )
        zw = sb("zw", [P, N], U32)
        zs = sb("zs", [P, N], U8)
        nc.vector.quantize_mx(out=zw[:].bitcast(FP8X4), scales=zs[:], in_=zg[:])

        z2g = sb("z2g", [P, N, PACK], BF16, "stage")
        for j in range(PACK - 1):
            nc.vector.tensor_scalar(z2g[:, :, j], dt[j][:], gb_t[:, j : j + 1], None, ALU.mult)
        for h in range(2):
            cols = slice(HALF * h, HALF * (h + 1))
            nc.vector.tensor_scalar(z2g[:, cols, PACK - 1], dt[PACK - 1][:, cols], gb_t[:, PACK - 1 : PACK], None, ALU.mult)
        z2w = sb("z2w", [P, N], U32)
        z2s = sb("z2s", [P, N], U8)
        for h in range(2):
            cols = slice(HALF * h, HALF * (h + 1))
            nc.vector.quantize_mx(
                out=z2w[:, cols].bitcast(FP8X4), scales=z2s[:, cols], in_=z2g[:, cols, :].rearrange("p c j -> p (c j)")
            )

        s_ps = []
        for t in range(PACK):
            bank = psum.tile([P, N], F32, name=f"s_ps{t}", tag=f"bs{t}")
            rows = slice(P * t, P * (t + 1))
            step = HALF if t == 0 else N
            for v0 in range(0, N, step):
                cols = slice(v0, v0 + step)
                nc.tensor.matmul_mx(
                    out=bank[:, cols], lhsT=zw[:, rows].bitcast(FP8X4), lhsT_scale=zs[:, rows],
                    rhs=z2w[:, cols].bitcast(FP8X4), rhs_scale=z2s[:, cols], start=True, stop=True,
                )
            s_ps.append(bank)
        sw = planes("sw", [P, N], F32)
        top = sb("top", [P, PACK], F32)
        shift = sb("shift", [P, PACK], F32)
        for t in range(PACK):
            nc.vector.tensor_scalar(sw[t][:], s_ps[t][:], 0.0625, None, ALU.mult, ALU.max, accum_out=top[:, t : t + 1])
            nc.vector.tensor_scalar(shift[:, t : t + 1], top[:, t : t + 1], tau_t[:, t : t + 1], -1.0, ALU.mult, ALU.mult)

        yw = sb("yw", [P, N], U32)
        ys = sb("ys", [P, N], U8)
        out_rows = out_0.rearrange("(p t) v -> p t v", t=PACK)
        out_words = out_1[0].rearrange("p c r -> p (c r)").bitcast(I32)
        def round_rows(copy, c, y, width):
            yg = sb(f"yg{c}", [P, width, PACK], BF16)
            copy(
                yg[:].rearrange("p (v i) t -> p v t i", i=4), y[:].rearrange("p t (v i) -> p v t i", i=4)
            )
            return yg

        def quantize_rows(yg, cols):
            nc.vector.quantize_mx(out=yw[:, cols].bitcast(FP8X4), scales=ys[:, cols], in_=yg[:].rearrange("p v t -> p (v t)"))
            nc.sync.dma_start(out_words[:, cols], yw[:, cols].bitcast(I32))

        c0 = 0
        last = None
        for c, width in enumerate(CHUNKS):
            cols = slice(c0, c0 + width)
            half = width // 2
            halves = [slice(0, half), slice(half, width)]
            ea = sb(f"ea{c}", [P, PACK, MEMBERS * width], F32)
            for e0 in range(0, width, EXP_COLS):
                for t in range(PACK):
                    lo = (c0 + e0) * MEMBERS // 16
                    nc.scalar.activation(
                        ea[:, t ^ 1, MEMBERS * e0 : MEMBERS * (e0 + EXP_COLS)],
                        sw[t][:].indirect(n5_t[:, lo : lo + EXP_COLS * MEMBERS // 16]),
                        ACT.Exp, bias=shift[:, t : t + 1], scale=tau_t[:, t : t + 1],
                    )
            pairs = sb(f"pairs{c}", [P, 2, PACK * half, 2], F32, "work")
            den = sb(f"den{c}", [P, 2, PACK, half], F32)
            d2 = sb(f"d2_{c}", [P, 2, 2, half], F32)
            d4 = sb(f"d4_{c}", [P, 2, half], F32)
            inv4 = sb(f"inv4_{c}", [P, 2, half], F32)
            inv2 = sb(f"inv2_{c}", [P, 2, 2, half], F32)
            y = sb(f"y{c}", [P, PACK, width], F32)

            def add_pairs(h):
                ea4 = ea[:].rearrange("p s (v a b) -> p s v a b", a=2, b=2)[:, :, halves[h], :, :]
                nc.vector.tensor_tensor(
                    pairs[:, h, :, :].rearrange("p (s v) b -> p s v b", s=PACK), ea4[:, :, :, 0, :], ea4[:, :, :, 1, :], ALU.add
                )

            def add_rest(h):
                nc.vector.scalar_tensor_tensor(
                    den[:, h, :, :].rearrange("p s v -> p (s v)"), pairs[:, h, :, 0], 0.5, pairs[:, h, :, 1], ALU.add, ALU.add
                )

            add_pairs(0)
            if last is not None:
                yg = round_rows(nc.scalar.copy if c == len(CHUNKS) - 1 else nc.vector.tensor_copy, *last[:3])
            add_rest(0)
            add_pairs(1)
            if last is not None:
                quantize_rows(yg, last[3])
            nc.vector.tensor_tensor(d2[:, 0, :, :], den[:, 0, 0:2, :], den[:, 0, 2:4, :], ALU.mult)
            add_rest(1)
            nc.vector.tensor_tensor(d4[:, 0, :], d2[:, 0, 0, :], d2[:, 0, 1, :], ALU.mult)
            num = sb(f"num{c}", [P, PACK, width], F32, "work")

            def numerator(t):
                nc.vector.scalar_tensor_tensor(
                    num[:, t, :].rearrange("p (h v) -> p h v", h=2),
                    s_ps[t][:, cols].rearrange("p (h v) -> p h v", h=2),
                    1.5 * 0.0625, den[:, :, t ^ 3, :], ALU.mult, ALU.mult,
                )

            def finish(h):
                nc.vector.tensor_tensor(
                    y[:, :, halves[h]].rearrange("p (u g) v -> p u g v", u=2),
                    num[:, :, halves[h]].rearrange("p (u g) v -> p u g v", u=2),
                    inv2[:, h, :, :].unsqueeze(1).to_broadcast([P, 2, 2, half]),
                    ALU.mult,
                )

            def spread(h):
                nc.vector.tensor_tensor(
                    inv2[:, h, :, :], d2[:, h, :, :], inv4[:, h, :].unsqueeze(1).to_broadcast([P, 2, half]), ALU.mult
                )

            nc.vector.tensor_tensor(d2[:, 1, :, :], den[:, 1, 0:2, :], den[:, 1, 2:4, :], ALU.mult)
            numerator(0)
            nc.vector.reciprocal(inv4[:, 0, :], d4[:, 0, :])
            nc.vector.tensor_tensor(d4[:, 1, :], d2[:, 1, 0, :], d2[:, 1, 1, :], ALU.mult)
            numerator(1)
            spread(0)
            nc.vector.reciprocal(inv4[:, 1, :], d4[:, 1, :])
            numerator(2)
            numerator(3)
            spread(1)
            finish(0)
            finish(1)
            nc.sync.dma_start(out_rows[:, :, cols], y[:])
            last = (c, y, width, cols)
            c0 = c0 + width
        quantize_rows(round_rows(nc.vector.tensor_copy, *last[:3]), last[3])
        for q in range(4):
            nc.scalar.dma_start(out_2[0, 4 * q : 4 * q + 4, :].bitcast(I32), ys[32 * q : 32 * q + 4, :].bitcast(I32))
